import numpy as np
import ml_dtypes


def mxq(x, axis, fmt="e4m3"):
    dtype, down = {"e4m3": (ml_dtypes.float8_e4m3fn, 7), "e5m2": (ml_dtypes.float8_e5m2, 14)}[fmt]
    v = np.moveaxis(np.asarray(x, np.float32).astype(ml_dtypes.bfloat16).astype(np.float64), axis, -1)
    blocks = v.reshape(v.shape[:-1] + (-1, 32))
    amax = np.abs(blocks).max(-1, keepdims=True)
    byte = np.maximum(np.where(amax > 0, np.frexp(amax)[1] - 1 + 127, 0) - down, 1)
    scale = np.exp2(byte - 127.0)
    codes = (blocks / scale).astype(np.float32).astype(dtype).astype(np.float64)
    return np.moveaxis((codes * scale).reshape(v.shape), -1, axis)


WIDE = False


def mx_kscale(k):
    if not WIDE:
        return np.ones(k)
    levels = np.array([10, -10, 5, -5, 0])
    if k % 512:
        return np.exp2(np.random.permutation(np.resize(levels, k // 32))).repeat(32)
    a = np.empty((k // 512, 16))
    for p in range(k // 512):
        a[p, :8] = np.random.permutation(np.resize(levels, 8))
        for g in range(8):
            far = levels[np.abs(levels - a[p, g]) >= 10]
            a[p, g + 8] = far[np.random.randint(len(far))]
    return np.exp2(a.ravel()).repeat(32)


def f64(x):
    return np.asarray(x).astype(np.float64)


def striped(idx):
    return np.tile(idx.reshape(-1, 16).T, (8, 1)).astype(np.uint16)


def unstriped(offs):
    return offs[:16].T.reshape(-1).astype(np.int64)


E2M1 = np.array([0.0, 0.5, 1.0, 1.5, 2.0, 3.0, 4.0, 6.0, -0.0, -0.5, -1.0, -1.5, -2.0, -3.0, -4.0, -6.0])


def pack_weight(w, fmt):
    k, n = w.shape
    w = f64(np.asarray(w, np.float32).astype(ml_dtypes.bfloat16)).reshape(k // 32, 32, n)
    amax = np.abs(w).max(1)
    if fmt == "e4m3":
        byte = np.frexp(amax)[1] - 1 + 127 - 7
    else:
        mant, ex = np.frexp(amax / 6.0)
        byte = np.where(mant > 0.5, ex, ex - 1) + 127
    byte = np.clip(np.where(amax > 0, byte, 1), 1, 254)
    scaled = (w * np.exp2(127.0 - byte)[:, None, :]).reshape(k, n).astype(np.float32)
    by_word = np.ascontiguousarray(scaled.reshape(k // 512, 128, 4, n).transpose(0, 1, 3, 2))
    if fmt == "e4m3":
        words = by_word.astype(ml_dtypes.float8_e4m3fn).view(np.uint8)
    else:
        c = by_word.astype(ml_dtypes.float4_e2m1fn).view(np.uint8) & 0xF
        words = (c[..., 0::2] | (c[..., 1::2] << 4)).reshape(k // 512, 128, 2 * n)
    return np.ascontiguousarray(words), np.ascontiguousarray(byte.astype(np.uint8).reshape(k // 512, 16, n))


def unpack_weight(words, scales, fmt):
    g, _, n = scales.shape
    words = np.ascontiguousarray(words).reshape(g, 128, n, -1)
    if fmt == "e4m3":
        vals = words.view(ml_dtypes.float8_e4m3fn).astype(np.float64)
    else:
        nib = np.empty((g, 128, n, 4), np.uint8)
        nib[..., 0::2] = words & 0xF
        nib[..., 1::2] = words >> 4
        vals = E2M1[nib]
    vals = vals * np.repeat(np.exp2(scales.astype(np.float64) - 127.0), 8, axis=1)[..., None]
    return vals.transpose(0, 1, 3, 2).reshape(g * 512, n)


def gelu(v):
    return 0.5 * v * (1.0 + np.tanh(np.sqrt(2.0 / np.pi) * (v + 0.044715 * v**3)))


K, T, S, P, H = 1536, 2048, 1024, 512, 512


def setup_inputs():
    n = np.random.standard_normal
    s = mx_kscale(K)[:, None]
    u = mx_kscale(H)[:, None]
    tab_words, tab_scales = pack_weight(n((K, T)) * s, "e4m3")
    w2_words, w2_scales = pack_weight(0.42 * n((K, H)) / np.sqrt(K) / s, "e2m1")
    perm = np.random.permutation(S)
    return {
        "tab_words": tab_words, "tab_scales": tab_scales,
        "offs": striped(np.random.permutation(T)[:S]),
        "pos1": striped(perm[:P]),
        "pos2": striped(perm[P:]),
        "w1": (0.53 * n((K, H)) / np.sqrt(K) / s).astype(np.float32),
        "w2_words": w2_words, "w2_scales": w2_scales,
        "amp": np.random.uniform(0.8, 1.5, H).astype(np.float32),
        "base": np.random.uniform(-0.4, 0.4, H).astype(np.float32),
        "temp": np.random.uniform(0.4, 1.6, H).astype(np.float32),
        "shift": (0.5 * n(H)).astype(np.float32),
        "mem": (0.4 * n((H, P))).astype(np.float32),
        "skip": np.random.uniform(0.5, 1.5, H).astype(np.float32),
        "wgs": np.exp(0.3 * n((128, P))).astype(np.float32),
        "gain": (np.random.uniform(0.5, 2.0, H) * u[:, 0]).astype(np.float32),
        "w3": (n((H, H)) / np.sqrt(H) / u).astype(np.float32),
        "resp": np.random.uniform(0.3, 1.5, (H, S)).astype(np.float32),
    }


def reference(tab_words, tab_scales, offs, pos1, pos2, w1, w2_words, w2_scales, amp, base,
              temp, shift, mem, skip, wgs, gain, w3, resp):
    v = unpack_weight(tab_words, tab_scales, "e4m3")[:, unstriped(offs)]
    wave = mxq(f64(w1), 0, "e4m3").T @ v
    line = unpack_weight(w2_words, w2_scales, "e2m1").T @ v
    h = f64(amp)[:, None] * np.sin(wave) + line + f64(base)[:, None]
    a = np.exp(f64(temp)[:, None] * h[:, unstriped(pos1)] + f64(shift)[:, None])
    a = a * f64(mem)
    page = f64(skip)[:, None] * h
    page[:, unstriped(pos2)] = np.tile(f64(wgs), (H // 128, 1)) * a
    z = mxq(f64(gain)[:, None] * page, 0, "e4m3")
    y = mxq(f64(w3), 0, "e4m3").T @ z
    return f64(resp) * y + h

@@ -1,0 +1,317 @@
+import math
+from contextlib import ExitStack
+
+import concourse.mybir as mybir
+
+K, T, S, PICK, H = 1536, 2048, 1024, 512, 512
+FLOPS = 2 * K * H * S * 2 + 2 * H * H * S
+
+F32 = mybir.dt.float32
+BF16 = mybir.dt.bfloat16
+I32 = mybir.dt.int32
+U32 = mybir.dt.uint32
+U16 = mybir.dt.uint16
+U8 = mybir.dt.uint8
+FP8X4 = mybir.dt.float8_e4m3fn_x4
+FP4X4 = mybir.dt.float4_e2m1fn_x4
+ACT = mybir.ActivationFunctionType
+ALU = mybir.AluOpType
+
+P = 128
+PACK = 4
+PASSES = K // (P * PACK)
+BANK = 512
+HALVES = S // BANK
+QUADS = 4
+SCALE_SPAN = 100
+SCALE_ROW0 = 32 - 4 * PASSES
+
+
+def tile_list_electrode_fouling_features_kernel(
+    tc, tab_words, tab_scales, offs, pos1, pos2, w1, w2_words, w2_scales, amp, base,
+    temp, shift, mem, skip, wgs, gain, w3, resp, out,
+):
+    nc = tc.nc
+    with ExitStack() as ctx:
+        keep = ctx.enter_context(tc.tile_pool(name="keep", bufs=1))
+        ring = ctx.enter_context(tc.tile_pool(name="ring", bufs=3))
+        psum = ctx.enter_context(tc.psum_pool(name="psum", bufs=1))
+
+        def bank(t, hf):
+            return psum.tile([P, BANK], F32, name=f"bank{t}{hf}")
+
+        def cols(hf):
+            return slice(hf * BANK, (hf + 1) * BANK)
+
+        def load_rows(rows):
+            raw = ring.tile([P, PACK, H], F32, name="big")
+            nc.sync.dma_start(out=raw[:], in_=rows.rearrange("(p j) c -> p j c", j=PACK))
+            return raw
+
+        def interleave(raw, copy):
+            grouped = ring.tile([P, PACK * H], BF16, name="grouped", align_bytes=64)
+            copy(
+                out=grouped[:].rearrange("p (t m j) -> p m j t", t=PACK, j=PACK),
+                in_=raw[:].rearrange("p j (m t) -> p m j t", t=PACK),
+            )
+            return grouped
+
+        def quantize(grouped, name):
+            codes = keep.tile([P, H], U32, name=f"{name}_codes", align_bytes=64)
+            scales = keep.tile([P, H], U8, name=f"{name}_scales", align_bytes=64)
+            nc.vector.quantize_mx(out=codes[:].bitcast(FP8X4), scales=scales[:], in_=grouped[:])
+            return codes, scales
+
+        def load_vector(vec, name):
+            col = keep.tile([P, PACK], F32, name=name)
+            nc.gpsimd.dma_start(out=col[:], in_=vec.rearrange("(p t) -> p t", t=PACK))
+            return col
+
+        def load_table(a):
+            words = ring.tile([P, T], I32, name="big")
+            nc.sync.dma_start(out=words[:], in_=tab_words[a].rearrange("p n i -> p (n i)").bitcast(I32))
+            return words
+
+        idx = keep.tile([P, S // 16], U16, name="idx")
+        nc.sync.dma_start(out=idx[:], in_=offs)
+        tab_sc = keep.tile([P, T], U8, name="tab_sc")
+        w1_raw = [load_rows(w1[0:512, :])]
+        w2_raw = keep.tile([P, PASSES, 2 * H], U8, name="w2_raw")
+        nc.sync.dma_start(out=w2_raw[:].bitcast(I32), in_=w2_words.rearrange("a p c -> p a c").bitcast(I32))
+        for q in range(QUADS):
+            nc.sync.dma_start(
+                out=tab_sc[32 * q + SCALE_ROW0 : 32 * q + 32, :].bitcast(I32),
+                in_=tab_scales[:, 4 * q : 4 * q + 4, :].bitcast(I32),
+            )
+            nc.vector.memset(tab_sc[32 * q : 32 * q + SCALE_ROW0, :].bitcast(I32), 0)
+        w1_raw.append(load_rows(w1[512:1024, :]))
+        w1_raw.append(load_rows(w1[1024:1536, :]))
+
+        w2_sc_raw = keep.tile([P, PASSES, H], U8, name="w2_sc_raw")
+        nc.gpsimd.memset(w2_sc_raw[:].bitcast(I32), 0)
+        for q in range(QUADS):
+            nc.sync.dma_start(
+                out=w2_sc_raw[32 * q : 32 * q + 4, :, :].bitcast(I32),
+                in_=w2_scales[:, 4 * q : 4 * q + 4, :].rearrange("a r c -> r a c").bitcast(I32),
+            )
+        v_planes = keep.tile([P, PASSES, S], U8, name="v_planes", align_bytes=64)
+        nc.vector.memset(v_planes[96:P, :, :].bitcast(I32), 0)
+        amp_c = load_vector(amp, "amp_c")
+        base_c = load_vector(base, "base_c")
+
+        phase = keep.tile([P, 1], F32, name="phase")
+        nc.vector.memset(phase[:], 1.0)
+        nc.vector.tensor_scalar(phase[:], phase[:], -math.pi / 4, None, ALU.mult)
+
+        v_sc = keep.tile([P, S], U8, name="v_sc", align_bytes=64)
+        nc.vector.tensor_copy(out=v_sc[:], in_=tab_sc[:].indirect(idx[:]))
+        for a in range(PASSES):
+            row0 = SCALE_ROW0 + 4 * a
+            nc.sync.dma_start(
+                out=v_planes[0:SCALE_SPAN, a, :].bitcast(I32),
+                in_=v_sc[row0 : row0 + SCALE_SPAN, :].bitcast(I32),
+            )
+        temp_c = load_vector(temp, "temp_c")
+        shift_c = load_vector(shift, "shift_c")
+        skip_c = load_vector(skip, "skip_c")
+        gain_c = load_vector(gain, "gain_c")
+
+        v_words = [keep.tile([P, S], I32, name=f"v{a}", align_bytes=64) for a in range(PASSES)]
+
+        def gather_words(a, lo, hi):
+            nc.vector.tensor_copy(
+                out=v_words[a][:, lo:hi].bitcast(U32),
+                in_=tab[a][:].bitcast(U32).indirect(idx[:, lo // 16 : hi // 16]),
+            )
+
+        wave = {(t, hf): bank(t, hf) for t in range(PACK) for hf in range(HALVES)}
+
+        def wave_pass(a, t, hf, w1_q):
+            codes, scales = w1_q
+            nc.tensor.matmul_mx(
+                out=wave[t, hf][:],
+                lhsT=codes[:, t * P : (t + 1) * P].bitcast(FP8X4),
+                lhsT_scale=scales[:, t * P : (t + 1) * P],
+                rhs=v_words[a][:, cols(hf)].bitcast(FP8X4),
+                rhs_scale=v_planes[:, a, cols(hf)],
+                start=(a == 0),
+                stop=(a == PASSES - 1),
+            )
+
+        w2_codes = keep.tile([P, PASSES, 2 * H], U8, name="w2_codes", align_bytes=64)
+        w2_sc = keep.tile([P, PASSES, H], U8, name="w2_sc", align_bytes=64)
+        slope = keep.tile([P, PACK], F32, name="slope")
+        level = keep.tile([P, PACK], F32, name="level")
+
+        last = PASSES - 1
+        tab = []
+        w1_all = []
+        for a in range(PASSES):
+            grouped = interleave(w1_raw[a], nc.scalar.copy)
+            tab.append(load_table(a))
+            w1_all.append(quantize(grouped, f"w1_{a}"))
+        nc.scalar.copy(
+            out=w2_codes[:].bitcast(U16).rearrange("p a (t m) -> p a t m", t=PACK),
+            in_=w2_raw[:].bitcast(U16).rearrange("p a (m t) -> p a t m", t=PACK),
+        )
+        nc.vector.tensor_scalar(slope[:], amp_c[:], -2.0, None, ALU.mult)
+        nc.vector.tensor_tensor(level[:], amp_c[:], base_c[:], ALU.add)
+        nc.vector.tensor_copy(
+            out=w2_sc[:].rearrange("p a (t m) -> p a t m", t=PACK),
+            in_=w2_sc_raw[:].rearrange("p a (m t) -> p a t m", t=PACK),
+        )
+        for a in range(last):
+            for hf in range(HALVES):
+                gather_words(a, hf * BANK, (hf + 1) * BANK)
+                for t in range(PACK):
+                    wave_pass(a, t, hf, w1_all[a])
+        w1_q = w1_all[last]
+        p1 = keep.tile([P, PICK // 16], U16, name="p1")
+        nc.sync.dma_start(out=p1[:], in_=pos1)
+        p2 = keep.tile([P, PICK // 16], U16, name="p2")
+        nc.sync.dma_start(out=p2[:], in_=pos2)
+        mem_t = ring.tile([P, PACK, PICK], F32, name="big")
+        nc.sync.dma_start(out=mem_t[:], in_=mem.rearrange("(p t) m -> p t m", t=PACK))
+        wgs_t = ring.tile([P, PACK, PICK], F32, name="big")
+        for q in range(QUADS):
+            nc.sync.dma_start(out=wgs_t[32 * q : 32 * q + 32, :, :], in_=wgs.rearrange("(p t) m -> p t m", t=PACK))
+
+        sine = [keep.tile([P, S], F32, name=f"sine{t}") for t in range(PACK)]
+        for hf in range(HALVES):
+            gather_words(last, hf * BANK, (hf + 1) * BANK)
+            for t in range(PACK):
+                wave_pass(last, t, hf, w1_q)
+        for t0 in range(0, PACK, 2):
+            for hf in range(HALVES):
+                for t in (t0, t0 + 1):
+                    nc.scalar.activation(
+                        out=sine[t][:, cols(hf)], in_=wave[t, hf][:], func=ACT.Sin, bias=phase[:], scale=0.5
+                    )
+
+        w3_raw = load_rows(w3)
+        line = {}
+        for t in range(PACK):
+            for hf in range(HALVES):
+                line[t, hf] = bank(t, hf)
+                for a in range(PASSES):
+                    nc.tensor.matmul_mx(
+                        out=line[t, hf][:],
+                        lhsT=w2_codes[:, a, 2 * t * P : 2 * (t + 1) * P].bitcast(FP4X4),
+                        lhsT_scale=w2_sc[:, a, t * P : (t + 1) * P],
+                        rhs=v_words[a][:, cols(hf)].bitcast(FP8X4),
+                        rhs_scale=v_planes[:, a, cols(hf)],
+                        start=(a == 0),
+                        stop=(a == last),
+                    )
+
+        h = [keep.tile([P, S], F32, name=f"h{t}") for t in range(PACK)]
+        page = [keep.tile([P, S], F32, name=f"page{t}") for t in range(PACK)]
+        look = [keep.tile([P, PICK], F32, name=f"look{t}") for t in range(PACK)]
+        rounded = keep.tile([P, PACK, S], BF16, name="rounded")
+
+        def features_on_vector(t):
+            for hf in range(HALVES):
+                s = sine[t][:, cols(hf)]
+                nc.vector.scalar_tensor_tensor(s, s, slope[:, t : t + 1], s, ALU.mult, ALU.mult)
+                nc.vector.scalar_tensor_tensor(
+                    h[t][:, cols(hf)], s, level[:, t : t + 1], line[t, hf][:], ALU.add, ALU.add
+                )
+
+        def periodic_on_scalar(t):
+            nc.scalar.activation(out=sine[t][:], in_=sine[t][:], func=ACT.Square)
+            nc.scalar.activation(
+                out=sine[t][:], in_=sine[t][:], func=ACT.Identity,
+                bias=level[:, t : t + 1], scale=slope[:, t : t + 1],
+            )
+
+        def add_line(t):
+            for hf in range(HALVES):
+                nc.vector.tensor_tensor(h[t][:, cols(hf)], line[t, hf][:], sine[t][:, cols(hf)], ALU.add)
+
+        resp_t = []
+
+        def load_resp(t):
+            resp_t.append(keep.tile([P, S], F32, name=f"sine{t}"))
+            nc.sync.dma_start(out=resp_t[t][:], in_=resp.rearrange("(p t) j -> p t j", t=PACK)[:, t, :])
+
+        def take_look(t):
+            nc.scalar.activation(
+                out=look[t][:], in_=h[t][:].indirect(p1[:]), func=ACT.Exp,
+                bias=shift_c[:, t : t + 1], scale=temp_c[:, t : t + 1],
+            )
+
+        def fill_page_on_scalar(t):
+            nc.scalar.activation(out=page[t][:], in_=h[t][:], func=ACT.Copy, scale=skip_c[:, t : t + 1])
+
+        def weights(t):
+            nc.vector.tensor_tensor(mem_t[:, t, :], mem_t[:, t, :], wgs_t[:, t, :], ALU.mult)
+
+        def put(t):
+            nc.vector.tensor_tensor(page[t][:].indirect(p2[:]), look[t][:], mem_t[:, t, :], ALU.mult)
+
+        def round_on_scalar(t):
+            nc.scalar.activation(out=rounded[:, t, :], in_=page[t][:], func=ACT.Copy, scale=gain_c[:, t : t + 1])
+
+        features_on_vector(0)
+        load_resp(0)
+        take_look(0)
+        nc.vector.tensor_scalar(page[0][:], h[0][:], skip_c[:, 0:1], None, ALU.mult)
+        features_on_vector(1)
+        load_resp(1)
+        weights(0)
+        put(0)
+        periodic_on_scalar(2)
+        take_look(1)
+        fill_page_on_scalar(1)
+        add_line(2)
+        load_resp(2)
+        weights(1)
+        put(1)
+        periodic_on_scalar(3)
+        take_look(2)
+        fill_page_on_scalar(2)
+        add_line(3)
+        load_resp(3)
+        weights(2)
+        put(2)
+        round_on_scalar(0)
+        take_look(3)
+        fill_page_on_scalar(3)
+        weights(3)
+        round_on_scalar(1)
+        w3_grouped = interleave(w3_raw, nc.scalar.copy)
+        put(3)
+        round_on_scalar(2)
+        w3_codes, w3_sc = quantize(w3_grouped, "w3")
+        nc.vector.tensor_scalar(rounded[:, 3, cols(0)], page[3][:, cols(0)], gain_c[:, 3:4], None, ALU.mult)
+        nc.scalar.activation(out=rounded[:, 3, cols(1)], in_=page[3][:, cols(1)], func=ACT.Copy, scale=gain_c[:, 3:4])
+
+        out_v = out.rearrange("(p t) j -> p t j", t=PACK)
+        z_q = []
+        for hf, copy in ((0, nc.vector.tensor_copy), (1, nc.scalar.copy)):
+            woven = ring.tile([P, PACK * BANK], BF16, name="grouped", align_bytes=64)
+            copy(
+                out=woven[:].rearrange("p (c i t) -> p c t i", i=4, t=PACK),
+                in_=rounded[:, :, cols(hf)].rearrange("p t (c i) -> p c t i", i=4),
+            )
+            z_q.append(woven)
+        for hf in range(HALVES):
+            z_codes, z_sc = quantize(z_q[hf], f"z{hf}")
+            readout = [bank(t, hf) for t in range(PACK)]
+            for t in range(PACK):
+                nc.tensor.matmul_mx(
+                    out=readout[t][:],
+                    lhsT=w3_codes[:, t * P : (t + 1) * P].bitcast(FP8X4),
+                    lhsT_scale=w3_sc[:, t * P : (t + 1) * P],
+                    rhs=z_codes[:].bitcast(FP8X4),
+                    rhs_scale=z_sc[:],
+                    start=True,
+                    stop=True,
+                )
+            for t in range(PACK):
+                res = resp_t[t][:, cols(hf)]
+                nc.vector.tensor_tensor(res, readout[t][:], res, ALU.mult)
+            for t in range(PACK):
+                res = resp_t[t][:, cols(hf)]
+                nc.vector.tensor_tensor(res, res, h[t][:, cols(hf)], ALU.add)
+                nc.sync.dma_start(out=out_v[:, t, cols(hf)], in_=res)

@@ -24,6 +24,7 @@ BANK = 512
 HALVES = S // BANK
 QUADS = 4
 SCALE_SPAN = 100
+SPLIT = 704
 SCALE_ROW0 = 32 - 4 * PASSES
 
 
@@ -48,11 +49,12 @@ def tile_list_electrode_fouling_features_kernel(
             nc.sync.dma_start(out=raw[:], in_=rows.rearrange("(p j) c -> p j c", j=PACK))
             return raw
 
-        def interleave(raw, copy):
-            grouped = ring.tile([P, PACK * H], BF16, name="grouped", align_bytes=64)
+        def interleave(raw, copy, grouped=None, lo=0, hi=P):
+            if grouped is None:
+                grouped = ring.tile([P, PACK * H], BF16, name="grouped", align_bytes=64)
             copy(
-                out=grouped[:].rearrange("p (t m j) -> p m j t", t=PACK, j=PACK),
-                in_=raw[:].rearrange("p j (m t) -> p m j t", t=PACK),
+                out=grouped[:].rearrange("p (t m j) -> p m j t", t=PACK, j=PACK)[:, lo:hi],
+                in_=raw[:].rearrange("p j (m t) -> p m j t", t=PACK)[:, lo:hi],
             )
             return grouped
 
@@ -85,7 +87,6 @@ def tile_list_electrode_fouling_features_kernel(
             )
             nc.vector.memset(tab_sc[32 * q : 32 * q + SCALE_ROW0, :].bitcast(I32), 0)
         w1_raw.append(load_rows(w1[512:1024, :]))
-        w1_raw.append(load_rows(w1[1024:1536, :]))
 
         w2_sc_raw = keep.tile([P, PASSES, H], U8, name="w2_sc_raw")
         nc.gpsimd.memset(w2_sc_raw[:].bitcast(I32), 0)
@@ -94,8 +95,7 @@ def tile_list_electrode_fouling_features_kernel(
                 out=w2_sc_raw[32 * q : 32 * q + 4, :, :].bitcast(I32),
                 in_=w2_scales[:, 4 * q : 4 * q + 4, :].rearrange("a r c -> r a c").bitcast(I32),
             )
-        v_planes = keep.tile([P, PASSES, S], U8, name="v_planes", align_bytes=64)
-        nc.vector.memset(v_planes[96:P, :, :].bitcast(I32), 0)
+        tab = [load_table(0)]
         amp_c = load_vector(amp, "amp_c")
         base_c = load_vector(base, "base_c")
 
@@ -105,12 +105,8 @@ def tile_list_electrode_fouling_features_kernel(
 
         v_sc = keep.tile([P, S], U8, name="v_sc", align_bytes=64)
         nc.vector.tensor_copy(out=v_sc[:], in_=tab_sc[:].indirect(idx[:]))
-        for a in range(PASSES):
-            row0 = SCALE_ROW0 + 4 * a
-            nc.sync.dma_start(
-                out=v_planes[0:SCALE_SPAN, a, :].bitcast(I32),
-                in_=v_sc[row0 : row0 + SCALE_SPAN, :].bitcast(I32),
-            )
+        v_packed = keep.tile([P, S], U8, name="v_packed", align_bytes=64)
+        nc.sync.dma_start(out=v_packed[0 : P - SCALE_ROW0, :].bitcast(I32), in_=v_sc[SCALE_ROW0:P, :].bitcast(I32))
         temp_c = load_vector(temp, "temp_c")
         shift_c = load_vector(shift, "shift_c")
         skip_c = load_vector(skip, "skip_c")
@@ -133,7 +129,7 @@ def tile_list_electrode_fouling_features_kernel(
                 lhsT=codes[:, t * P : (t + 1) * P].bitcast(FP8X4),
                 lhsT_scale=scales[:, t * P : (t + 1) * P],
                 rhs=v_words[a][:, cols(hf)].bitcast(FP8X4),
-                rhs_scale=v_planes[:, a, cols(hf)],
+                rhs_scale=v_packed[4 * a : P, cols(hf)],
                 start=(a == 0),
                 stop=(a == PASSES - 1),
             )
@@ -144,12 +140,12 @@ def tile_list_electrode_fouling_features_kernel(
         level = keep.tile([P, PACK], F32, name="level")
 
         last = PASSES - 1
-        tab = []
-        w1_all = []
-        for a in range(PASSES):
-            grouped = interleave(w1_raw[a], nc.scalar.copy)
-            tab.append(load_table(a))
-            w1_all.append(quantize(grouped, f"w1_{a}"))
+        grouped = interleave(w1_raw[0], nc.scalar.copy)
+        w1_raw.append(load_rows(w1[1024:1536, :]))
+        w1_all = [quantize(grouped, "w1_0")]
+        grouped = interleave(w1_raw[1], nc.scalar.copy)
+        tab.append(load_table(1))
+        w1_all.append(quantize(grouped, "w1_1"))
         nc.scalar.copy(
             out=w2_codes[:].bitcast(U16).rearrange("p a (t m) -> p a t m", t=PACK),
             in_=w2_raw[:].bitcast(U16).rearrange("p a (m t) -> p a t m", t=PACK),
@@ -160,12 +156,27 @@ def tile_list_electrode_fouling_features_kernel(
             out=w2_sc[:].rearrange("p a (t m) -> p a t m", t=PACK),
             in_=w2_sc_raw[:].rearrange("p a (m t) -> p a t m", t=PACK),
         )
-        for a in range(last):
+
+        def early_pass(a):
             for hf in range(HALVES):
                 gather_words(a, hf * BANK, (hf + 1) * BANK)
                 for t in range(PACK):
                     wave_pass(a, t, hf, w1_all[a])
-        w1_q = w1_all[last]
+
+        early_pass(0)
+        tab.append(load_table(2))
+        grouped = keep.tile([P, PACK * H], BF16, name="shared", align_bytes=64)
+        interleave(w1_raw[last], nc.scalar.copy, grouped, 0, P // 2)
+        interleave(w1_raw[last], nc.vector.tensor_copy, grouped, P // 2, P)
+        w1_q = quantize(grouped, "w1_2")
+        early_pass(1)
+        v_planes = keep.tile([P, PASSES - 1, S], U8, name="shared", align_bytes=64)
+        for a in range(1, PASSES):
+            row0 = SCALE_ROW0 + 4 * a
+            nc.sync.dma_start(
+                out=v_planes[0:SCALE_SPAN, a - 1, :].bitcast(I32),
+                in_=v_sc[row0 : row0 + SCALE_SPAN, :].bitcast(I32),
+            )
         p1 = keep.tile([P, PICK // 16], U16, name="p1")
         nc.sync.dma_start(out=p1[:], in_=pos1)
         p2 = keep.tile([P, PICK // 16], U16, name="p2")
@@ -173,7 +184,7 @@ def tile_list_electrode_fouling_features_kernel(
         mem_t = ring.tile([P, PACK, PICK], F32, name="big")
         nc.sync.dma_start(out=mem_t[:], in_=mem.rearrange("(p t) m -> p t m", t=PACK))
         wgs_t = ring.tile([P, PACK, PICK], F32, name="big")
-        for q in range(QUADS):
+        for q in (0, 2, 1, 3):
             nc.sync.dma_start(out=wgs_t[32 * q : 32 * q + 32, :, :], in_=wgs.rearrange("(p t) m -> p t m", t=PACK))
 
         sine = [keep.tile([P, S], F32, name=f"sine{t}") for t in range(PACK)]
@@ -199,14 +210,14 @@ def tile_list_electrode_fouling_features_kernel(
                         lhsT=w2_codes[:, a, 2 * t * P : 2 * (t + 1) * P].bitcast(FP4X4),
                         lhsT_scale=w2_sc[:, a, t * P : (t + 1) * P],
                         rhs=v_words[a][:, cols(hf)].bitcast(FP8X4),
-                        rhs_scale=v_planes[:, a, cols(hf)],
+                        rhs_scale=v_packed[:, cols(hf)] if a == 0 else v_planes[:, a - 1, cols(hf)],
                         start=(a == 0),
                         stop=(a == last),
                     )
 
-        h = [keep.tile([P, S], F32, name=f"h{t}") for t in range(PACK)]
         page = [keep.tile([P, S], F32, name=f"page{t}") for t in range(PACK)]
-        look = [keep.tile([P, PICK], F32, name=f"look{t}") for t in range(PACK)]
+        h = {t: keep.tile([P, S], F32, name=f"h{t}") for t in (0, 1)}
+        look = {}
         rounded = keep.tile([P, PACK, S], BF16, name="rounded")
 
         def features_on_vector(t):
@@ -225,6 +236,7 @@ def tile_list_electrode_fouling_features_kernel(
             )
 
         def add_line(t):
+            h[t] = keep.tile([P, S], F32, name=f"h{t}")
             for hf in range(HALVES):
                 nc.vector.tensor_tensor(h[t][:, cols(hf)], line[t, hf][:], sine[t][:, cols(hf)], ALU.add)
 
@@ -235,6 +247,7 @@ def tile_list_electrode_fouling_features_kernel(
             nc.sync.dma_start(out=resp_t[t][:], in_=resp.rearrange("(p t) j -> p t j", t=PACK)[:, t, :])
 
         def take_look(t):
+            look[t] = keep.tile([P, PICK], F32, name=f"h{t + 2}")
             nc.scalar.activation(
                 out=look[t][:], in_=h[t][:].indirect(p1[:]), func=ACT.Exp,
                 bias=shift_c[:, t : t + 1], scale=temp_c[:, t : t + 1],
@@ -274,44 +287,55 @@ def tile_list_electrode_fouling_features_kernel(
         load_resp(3)
         weights(2)
         put(2)
-        round_on_scalar(0)
         take_look(3)
         fill_page_on_scalar(3)
+        round_on_scalar(0)
         weights(3)
         round_on_scalar(1)
         w3_grouped = interleave(w3_raw, nc.scalar.copy)
         put(3)
         round_on_scalar(2)
         w3_codes, w3_sc = quantize(w3_grouped, "w3")
-        nc.vector.tensor_scalar(rounded[:, 3, cols(0)], page[3][:, cols(0)], gain_c[:, 3:4], None, ALU.mult)
-        nc.scalar.activation(out=rounded[:, 3, cols(1)], in_=page[3][:, cols(1)], func=ACT.Copy, scale=gain_c[:, 3:4])
+
+        woven = [ring.tile([P, PACK * BANK], BF16, name="grouped", align_bytes=64) for hf in range(HALVES)]
+
+        def weave(lo, hi, copy):
+            hf = lo // BANK
+            copy(
+                out=woven[hf][:, PACK * (lo - hf * BANK) : PACK * (hi - hf * BANK)].rearrange(
+                    "p (c i t) -> p c t i", i=4, t=PACK
+                ),
+                in_=rounded[:, :, lo:hi].rearrange("p t (c i) -> p c t i", i=4),
+            )
+
+        nc.vector.tensor_scalar(rounded[:, 3, :SPLIT], page[3][:, :SPLIT], gain_c[:, 3:4], None, ALU.mult)
+        nc.scalar.activation(out=rounded[:, 3, SPLIT:], in_=page[3][:, SPLIT:], func=ACT.Copy, scale=gain_c[:, 3:4])
+        weave(SPLIT, S, nc.scalar.copy)
+        weave(0, BANK, nc.vector.tensor_copy)
+        z_q = [quantize(woven[0], "z0")]
+        weave(BANK, SPLIT, nc.vector.tensor_copy)
+        z_q.append(quantize(woven[1], "z1"))
 
         out_v = out.rearrange("(p t) j -> p t j", t=PACK)
-        z_q = []
-        for hf, copy in ((0, nc.vector.tensor_copy), (1, nc.scalar.copy)):
-            woven = ring.tile([P, PACK * BANK], BF16, name="grouped", align_bytes=64)
-            copy(
-                out=woven[:].rearrange("p (c i t) -> p c t i", i=4, t=PACK),
-                in_=rounded[:, :, cols(hf)].rearrange("p t (c i) -> p c t i", i=4),
+        units = [(t, hf) for hf in range(HALVES) for t in range(PACK)]
+        readout = {}
+        for t, hf in units:
+            z_codes, z_sc = z_q[hf]
+            readout[t, hf] = bank(t, hf)
+            nc.tensor.matmul_mx(
+                out=readout[t, hf][:],
+                lhsT=w3_codes[:, t * P : (t + 1) * P].bitcast(FP8X4),
+                lhsT_scale=w3_sc[:, t * P : (t + 1) * P],
+                rhs=z_codes[:].bitcast(FP8X4),
+                rhs_scale=z_sc[:],
+                start=True,
+                stop=True,
             )
-            z_q.append(woven)
-        for hf in range(HALVES):
-            z_codes, z_sc = quantize(z_q[hf], f"z{hf}")
-            readout = [bank(t, hf) for t in range(PACK)]
-            for t in range(PACK):
-                nc.tensor.matmul_mx(
-                    out=readout[t][:],
-                    lhsT=w3_codes[:, t * P : (t + 1) * P].bitcast(FP8X4),
-                    lhsT_scale=w3_sc[:, t * P : (t + 1) * P],
-                    rhs=z_codes[:].bitcast(FP8X4),
-                    rhs_scale=z_sc[:],
-                    start=True,
-                    stop=True,
-                )
-            for t in range(PACK):
-                res = resp_t[t][:, cols(hf)]
-                nc.vector.tensor_tensor(res, readout[t][:], res, ALU.mult)
-            for t in range(PACK):
-                res = resp_t[t][:, cols(hf)]
-                nc.vector.tensor_tensor(res, res, h[t][:, cols(hf)], ALU.add)
-                nc.sync.dma_start(out=out_v[:, t, cols(hf)], in_=res)
+        for t, hf in units:
+            res = resp_t[t][:, cols(hf)]
+            nc.vector.tensor_tensor(res, readout[t, hf][:], res, ALU.mult)
+        for t, hf in units:
+            res = resp_t[t][:, cols(hf)]
+            adder = nc.gpsimd if hf == 0 else nc.vector
+            adder.tensor_tensor(res, res, h[t][:, cols(hf)], ALU.add)
+            nc.sync.dma_start(out=out_v[:, t, cols(hf)], in_=res)

import math
from contextlib import ExitStack

import concourse.mybir as mybir

K, T, S, PICK, H = 1536, 2048, 1024, 512, 512
FLOPS = 2 * K * H * S * 2 + 2 * H * H * S

F32 = mybir.dt.float32
BF16 = mybir.dt.bfloat16
I32 = mybir.dt.int32
U32 = mybir.dt.uint32
U16 = mybir.dt.uint16
U8 = mybir.dt.uint8
FP8X4 = mybir.dt.float8_e4m3fn_x4
FP4X4 = mybir.dt.float4_e2m1fn_x4
ACT = mybir.ActivationFunctionType
ALU = mybir.AluOpType

P = 128
PACK = 4
PASSES = K // (P * PACK)
BANK = 512
HALVES = S // BANK
QUADS = 4
SCALE_SPAN = 100
SPLIT = 704
SCALE_ROW0 = 32 - 4 * PASSES


def tile_list_electrode_fouling_features_kernel(
    tc, tab_words, tab_scales, offs, pos1, pos2, w1, w2_words, w2_scales, amp, base,
    temp, shift, mem, skip, wgs, gain, w3, resp, out,
):
    nc = tc.nc
    with ExitStack() as ctx:
        keep = ctx.enter_context(tc.tile_pool(name="keep", bufs=1))
        ring = ctx.enter_context(tc.tile_pool(name="ring", bufs=3))
        psum = ctx.enter_context(tc.psum_pool(name="psum", bufs=1))

        def bank(t, hf):
            return psum.tile([P, BANK], F32, name=f"bank{t}{hf}")

        def cols(hf):
            return slice(hf * BANK, (hf + 1) * BANK)

        def load_rows(rows):
            raw = ring.tile([P, PACK, H], F32, name="big")
            nc.sync.dma_start(out=raw[:], in_=rows.rearrange("(p j) c -> p j c", j=PACK))
            return raw

        def interleave(raw, copy, grouped=None, lo=0, hi=P):
            if grouped is None:
                grouped = ring.tile([P, PACK * H], BF16, name="grouped", align_bytes=64)
            copy(
                out=grouped[:].rearrange("p (t m j) -> p m j t", t=PACK, j=PACK)[:, lo:hi],
                in_=raw[:].rearrange("p j (m t) -> p m j t", t=PACK)[:, lo:hi],
            )
            return grouped

        def quantize(grouped, name):
            codes = keep.tile([P, H], U32, name=f"{name}_codes", align_bytes=64)
            scales = keep.tile([P, H], U8, name=f"{name}_scales", align_bytes=64)
            nc.vector.quantize_mx(out=codes[:].bitcast(FP8X4), scales=scales[:], in_=grouped[:])
            return codes, scales

        def load_vector(vec, name):
            col = keep.tile([P, PACK], F32, name=name)
            nc.gpsimd.dma_start(out=col[:], in_=vec.rearrange("(p t) -> p t", t=PACK))
            return col

        def load_table(a):
            words = ring.tile([P, T], I32, name="big")
            nc.sync.dma_start(out=words[:], in_=tab_words[a].rearrange("p n i -> p (n i)").bitcast(I32))
            return words

        idx = keep.tile([P, S // 16], U16, name="idx")
        nc.sync.dma_start(out=idx[:], in_=offs)
        tab_sc = keep.tile([P, T], U8, name="tab_sc")
        w1_raw = [load_rows(w1[0:512, :])]
        w2_raw = keep.tile([P, PASSES, 2 * H], U8, name="w2_raw")
        nc.sync.dma_start(out=w2_raw[:].bitcast(I32), in_=w2_words.rearrange("a p c -> p a c").bitcast(I32))
        for q in range(QUADS):
            nc.sync.dma_start(
                out=tab_sc[32 * q + SCALE_ROW0 : 32 * q + 32, :].bitcast(I32),
                in_=tab_scales[:, 4 * q : 4 * q + 4, :].bitcast(I32),
            )
            nc.vector.memset(tab_sc[32 * q : 32 * q + SCALE_ROW0, :].bitcast(I32), 0)
        w1_raw.append(load_rows(w1[512:1024, :]))

        w2_sc_raw = keep.tile([P, PASSES, H], U8, name="w2_sc_raw")
        nc.gpsimd.memset(w2_sc_raw[:].bitcast(I32), 0)
        for q in range(QUADS):
            nc.sync.dma_start(
                out=w2_sc_raw[32 * q : 32 * q + 4, :, :].bitcast(I32),
                in_=w2_scales[:, 4 * q : 4 * q + 4, :].rearrange("a r c -> r a c").bitcast(I32),
            )
        tab = [load_table(0)]
        amp_c = load_vector(amp, "amp_c")
        base_c = load_vector(base, "base_c")

        phase = keep.tile([P, 1], F32, name="phase")
        nc.vector.memset(phase[:], 1.0)
        nc.vector.tensor_scalar(phase[:], phase[:], -math.pi / 4, None, ALU.mult)

        v_sc = keep.tile([P, S], U8, name="v_sc", align_bytes=64)
        nc.vector.tensor_copy(out=v_sc[:], in_=tab_sc[:].indirect(idx[:]))
        v_packed = keep.tile([P, S], U8, name="v_packed", align_bytes=64)
        nc.sync.dma_start(out=v_packed[0 : P - SCALE_ROW0, :].bitcast(I32), in_=v_sc[SCALE_ROW0:P, :].bitcast(I32))
        temp_c = load_vector(temp, "temp_c")
        shift_c = load_vector(shift, "shift_c")
        skip_c = load_vector(skip, "skip_c")
        gain_c = load_vector(gain, "gain_c")

        v_words = [keep.tile([P, S], I32, name=f"v{a}", align_bytes=64) for a in range(PASSES)]

        def gather_words(a, lo, hi):
            nc.vector.tensor_copy(
                out=v_words[a][:, lo:hi].bitcast(U32),
                in_=tab[a][:].bitcast(U32).indirect(idx[:, lo // 16 : hi // 16]),
            )

        wave = {(t, hf): bank(t, hf) for t in range(PACK) for hf in range(HALVES)}

        def wave_pass(a, t, hf, w1_q):
            codes, scales = w1_q
            nc.tensor.matmul_mx(
                out=wave[t, hf][:],
                lhsT=codes[:, t * P : (t + 1) * P].bitcast(FP8X4),
                lhsT_scale=scales[:, t * P : (t + 1) * P],
                rhs=v_words[a][:, cols(hf)].bitcast(FP8X4),
                rhs_scale=v_packed[4 * a : P, cols(hf)],
                start=(a == 0),
                stop=(a == PASSES - 1),
            )

        w2_codes = keep.tile([P, PASSES, 2 * H], U8, name="w2_codes", align_bytes=64)
        w2_sc = keep.tile([P, PASSES, H], U8, name="w2_sc", align_bytes=64)
        slope = keep.tile([P, PACK], F32, name="slope")
        level = keep.tile([P, PACK], F32, name="level")

        last = PASSES - 1
        grouped = interleave(w1_raw[0], nc.scalar.copy)
        w1_raw.append(load_rows(w1[1024:1536, :]))
        w1_all = [quantize(grouped, "w1_0")]
        grouped = interleave(w1_raw[1], nc.scalar.copy)
        tab.append(load_table(1))
        w1_all.append(quantize(grouped, "w1_1"))
        nc.scalar.copy(
            out=w2_codes[:].bitcast(U16).rearrange("p a (t m) -> p a t m", t=PACK),
            in_=w2_raw[:].bitcast(U16).rearrange("p a (m t) -> p a t m", t=PACK),
        )
        nc.vector.tensor_scalar(slope[:], amp_c[:], -2.0, None, ALU.mult)
        nc.vector.tensor_tensor(level[:], amp_c[:], base_c[:], ALU.add)
        nc.vector.tensor_copy(
            out=w2_sc[:].rearrange("p a (t m) -> p a t m", t=PACK),
            in_=w2_sc_raw[:].rearrange("p a (m t) -> p a t m", t=PACK),
        )

        def early_pass(a):
            for hf in range(HALVES):
                gather_words(a, hf * BANK, (hf + 1) * BANK)
                for t in range(PACK):
                    wave_pass(a, t, hf, w1_all[a])

        early_pass(0)
        tab.append(load_table(2))
        grouped = keep.tile([P, PACK * H], BF16, name="shared", align_bytes=64)
        interleave(w1_raw[last], nc.scalar.copy, grouped, 0, P // 2)
        interleave(w1_raw[last], nc.vector.tensor_copy, grouped, P // 2, P)
        w1_q = quantize(grouped, "w1_2")
        early_pass(1)
        v_planes = keep.tile([P, PASSES - 1, S], U8, name="shared", align_bytes=64)
        for a in range(1, PASSES):
            row0 = SCALE_ROW0 + 4 * a
            nc.sync.dma_start(
                out=v_planes[0:SCALE_SPAN, a - 1, :].bitcast(I32),
                in_=v_sc[row0 : row0 + SCALE_SPAN, :].bitcast(I32),
            )
        p1 = keep.tile([P, PICK // 16], U16, name="p1")
        nc.sync.dma_start(out=p1[:], in_=pos1)
        p2 = keep.tile([P, PICK // 16], U16, name="p2")
        nc.sync.dma_start(out=p2[:], in_=pos2)
        mem_t = ring.tile([P, PACK, PICK], F32, name="big")
        nc.sync.dma_start(out=mem_t[:], in_=mem.rearrange("(p t) m -> p t m", t=PACK))
        wgs_t = ring.tile([P, PACK, PICK], F32, name="big")
        for q in (0, 2, 1, 3):
            nc.sync.dma_start(out=wgs_t[32 * q : 32 * q + 32, :, :], in_=wgs.rearrange("(p t) m -> p t m", t=PACK))

        sine = [keep.tile([P, S], F32, name=f"sine{t}") for t in range(PACK)]
        for hf in range(HALVES):
            gather_words(last, hf * BANK, (hf + 1) * BANK)
            for t in range(PACK):
                wave_pass(last, t, hf, w1_q)
        for t0 in range(0, PACK, 2):
            for hf in range(HALVES):
                for t in (t0, t0 + 1):
                    nc.scalar.activation(
                        out=sine[t][:, cols(hf)], in_=wave[t, hf][:], func=ACT.Sin, bias=phase[:], scale=0.5
                    )

        w3_raw = load_rows(w3)
        line = {}
        for t in range(PACK):
            for hf in range(HALVES):
                line[t, hf] = bank(t, hf)
                for a in range(PASSES):
                    nc.tensor.matmul_mx(
                        out=line[t, hf][:],
                        lhsT=w2_codes[:, a, 2 * t * P : 2 * (t + 1) * P].bitcast(FP4X4),
                        lhsT_scale=w2_sc[:, a, t * P : (t + 1) * P],
                        rhs=v_words[a][:, cols(hf)].bitcast(FP8X4),
                        rhs_scale=v_packed[:, cols(hf)] if a == 0 else v_planes[:, a - 1, cols(hf)],
                        start=(a == 0),
                        stop=(a == last),
                    )

        page = [keep.tile([P, S], F32, name=f"page{t}") for t in range(PACK)]
        h = {t: keep.tile([P, S], F32, name=f"h{t}") for t in (0, 1)}
        look = {}
        rounded = keep.tile([P, PACK, S], BF16, name="rounded")

        def features_on_vector(t):
            for hf in range(HALVES):
                s = sine[t][:, cols(hf)]
                nc.vector.scalar_tensor_tensor(s, s, slope[:, t : t + 1], s, ALU.mult, ALU.mult)
                nc.vector.scalar_tensor_tensor(
                    h[t][:, cols(hf)], s, level[:, t : t + 1], line[t, hf][:], ALU.add, ALU.add
                )

        def periodic_on_scalar(t):
            nc.scalar.activation(out=sine[t][:], in_=sine[t][:], func=ACT.Square)
            nc.scalar.activation(
                out=sine[t][:], in_=sine[t][:], func=ACT.Identity,
                bias=level[:, t : t + 1], scale=slope[:, t : t + 1],
            )

        def add_line(t):
            h[t] = keep.tile([P, S], F32, name=f"h{t}")
            for hf in range(HALVES):
                nc.vector.tensor_tensor(h[t][:, cols(hf)], line[t, hf][:], sine[t][:, cols(hf)], ALU.add)

        resp_t = []

        def load_resp(t):
            resp_t.append(keep.tile([P, S], F32, name=f"sine{t}"))
            nc.sync.dma_start(out=resp_t[t][:], in_=resp.rearrange("(p t) j -> p t j", t=PACK)[:, t, :])

        def take_look(t):
            look[t] = keep.tile([P, PICK], F32, name=f"h{t + 2}")
            nc.scalar.activation(
                out=look[t][:], in_=h[t][:].indirect(p1[:]), func=ACT.Exp,
                bias=shift_c[:, t : t + 1], scale=temp_c[:, t : t + 1],
            )

        def fill_page_on_scalar(t):
            nc.scalar.activation(out=page[t][:], in_=h[t][:], func=ACT.Copy, scale=skip_c[:, t : t + 1])

        def weights(t):
            nc.vector.tensor_tensor(mem_t[:, t, :], mem_t[:, t, :], wgs_t[:, t, :], ALU.mult)

        def put(t):
            nc.vector.tensor_tensor(page[t][:].indirect(p2[:]), look[t][:], mem_t[:, t, :], ALU.mult)

        def round_on_scalar(t):
            nc.scalar.activation(out=rounded[:, t, :], in_=page[t][:], func=ACT.Copy, scale=gain_c[:, t : t + 1])

        features_on_vector(0)
        load_resp(0)
        take_look(0)
        nc.vector.tensor_scalar(page[0][:], h[0][:], skip_c[:, 0:1], None, ALU.mult)
        features_on_vector(1)
        load_resp(1)
        weights(0)
        put(0)
        periodic_on_scalar(2)
        take_look(1)
        fill_page_on_scalar(1)
        add_line(2)
        load_resp(2)
        weights(1)
        put(1)
        periodic_on_scalar(3)
        take_look(2)
        fill_page_on_scalar(2)
        add_line(3)
        load_resp(3)
        weights(2)
        put(2)
        take_look(3)
        fill_page_on_scalar(3)
        round_on_scalar(0)
        weights(3)
        round_on_scalar(1)
        w3_grouped = interleave(w3_raw, nc.scalar.copy)
        put(3)
        round_on_scalar(2)
        w3_codes, w3_sc = quantize(w3_grouped, "w3")

        woven = [ring.tile([P, PACK * BANK], BF16, name="grouped", align_bytes=64) for hf in range(HALVES)]

        def weave(lo, hi, copy):
            hf = lo // BANK
            copy(
                out=woven[hf][:, PACK * (lo - hf * BANK) : PACK * (hi - hf * BANK)].rearrange(
                    "p (c i t) -> p c t i", i=4, t=PACK
                ),
                in_=rounded[:, :, lo:hi].rearrange("p t (c i) -> p c t i", i=4),
            )

        nc.vector.tensor_scalar(rounded[:, 3, :SPLIT], page[3][:, :SPLIT], gain_c[:, 3:4], None, ALU.mult)
        nc.scalar.activation(out=rounded[:, 3, SPLIT:], in_=page[3][:, SPLIT:], func=ACT.Copy, scale=gain_c[:, 3:4])
        weave(SPLIT, S, nc.scalar.copy)
        weave(0, BANK, nc.vector.tensor_copy)
        z_q = [quantize(woven[0], "z0")]
        weave(BANK, SPLIT, nc.vector.tensor_copy)
        z_q.append(quantize(woven[1], "z1"))

        out_v = out.rearrange("(p t) j -> p t j", t=PACK)
        units = [(t, hf) for hf in range(HALVES) for t in range(PACK)]
        readout = {}
        for t, hf in units:
            z_codes, z_sc = z_q[hf]
            readout[t, hf] = bank(t, hf)
            nc.tensor.matmul_mx(
                out=readout[t, hf][:],
                lhsT=w3_codes[:, t * P : (t + 1) * P].bitcast(FP8X4),
                lhsT_scale=w3_sc[:, t * P : (t + 1) * P],
                rhs=z_codes[:].bitcast(FP8X4),
                rhs_scale=z_sc[:],
                start=True,
                stop=True,
            )
        for t, hf in units:
            res = resp_t[t][:, cols(hf)]
            nc.vector.tensor_tensor(res, readout[t, hf][:], res, ALU.mult)
        for t, hf in units:
            res = resp_t[t][:, cols(hf)]
            adder = nc.gpsimd if hf == 0 else nc.vector
            adder.tensor_tensor(res, res, h[t][:, cols(hf)], ALU.add)
            nc.sync.dma_start(out=out_v[:, t, cols(hf)], in_=res)
